import numpy as np
import ml_dtypes


def mxq(x, axis, fmt="e4m3"):
    dtype, down = {"e4m3": (ml_dtypes.float8_e4m3fn, 7), "e5m2": (ml_dtypes.float8_e5m2, 14)}[fmt]
    v = np.moveaxis(np.asarray(x, np.float32).astype(ml_dtypes.bfloat16).astype(np.float64), axis, -1)
    blocks = v.reshape(v.shape[:-1] + (-1, 32))
    amax = np.abs(blocks).max(-1, keepdims=True)
    byte = np.maximum(np.where(amax > 0, np.frexp(amax)[1] - 1 + 127, 0) - down, 1)
    scale = np.exp2(byte - 127.0)
    codes = (blocks / scale).astype(np.float32).astype(dtype).astype(np.float64)
    return np.moveaxis((codes * scale).reshape(v.shape), -1, axis)


WIDE = False


def mx_kscale(k):
    if not WIDE:
        return np.ones(k)
    levels = np.array([10, -10, 5, -5, 0])
    if k % 512:
        return np.exp2(np.random.permutation(np.resize(levels, k // 32))).repeat(32)
    a = np.empty((k // 512, 16))
    for p in range(k // 512):
        a[p, :8] = np.random.permutation(np.resize(levels, 8))
        for g in range(8):
            far = levels[np.abs(levels - a[p, g]) >= 10]
            a[p, g + 8] = far[np.random.randint(len(far))]
    return np.exp2(a.ravel()).repeat(32)


BF16 = ml_dtypes.bfloat16


def bf(x):
    return np.asarray(x, np.float32).astype(BF16)


def f64(x):
    return np.asarray(x).astype(np.float64)


E2M1 = np.array([0.0, 0.5, 1.0, 1.5, 2.0, 3.0, 4.0, 6.0, -0.0, -0.5, -1.0, -1.5, -2.0, -3.0, -4.0, -6.0])


def pack_weight(w, fmt):
    k, n = w.shape
    w = f64(bf(w)).reshape(k // 32, 32, n)
    amax = np.abs(w).max(1)
    if fmt == "e4m3":
        byte = np.frexp(amax)[1] - 1 + 127 - 7
    else:
        mant, ex = np.frexp(amax / 6.0)
        byte = np.where(mant > 0.5, ex, ex - 1) + 127
    byte = np.clip(np.where(amax > 0, byte, 1), 1, 254)
    scaled = (w * np.exp2(127.0 - byte)[:, None, :]).reshape(k, n).astype(np.float32)
    by_word = np.ascontiguousarray(scaled.reshape(k // 512, 128, 4, n).transpose(0, 1, 3, 2))
    if fmt == "e4m3":
        words = by_word.astype(ml_dtypes.float8_e4m3fn).view(np.uint8)
    else:
        c = by_word.astype(ml_dtypes.float4_e2m1fn).view(np.uint8) & 0xF
        words = c[..., 0::2] | (c[..., 1::2] << 4)
    return np.ascontiguousarray(words), np.ascontiguousarray(byte.astype(np.uint8).reshape(k // 512, 16, n))


def unpack_weight(words, scales, fmt):
    g, p, n, _ = words.shape
    if fmt == "e4m3":
        vals = np.ascontiguousarray(words).view(ml_dtypes.float8_e4m3fn).astype(np.float64)
    else:
        nib = np.empty((g, p, n, 4), np.uint8)
        nib[..., 0::2] = words & 0xF
        nib[..., 1::2] = words >> 4
        vals = E2M1[nib]
    vals = vals * np.repeat(np.exp2(scales.astype(np.float64) - 127.0), 8, axis=1)[..., None]
    return vals.transpose(0, 1, 3, 2).reshape(g * 512, n)
def pack4(w):
    words, scales = pack_weight(w, "e2m1")
    return words.reshape(words.shape[0], 128, -1), scales


def unpack4(words, scales):
    return unpack_weight(words.reshape(words.shape[0], 128, -1, 2), scales, "e2m1")


E4M3FN = np.array([(-1.0 if i & 128 else 1.0) * ((1.0 + (i & 7) / 8.0) * 2.0 ** (((i >> 3) & 15) - 7) if i & 120 else (i & 7) * 2.0 ** -9) for i in range(256)])


def e4m3fn_bytes(y):
    return np.clip(np.asarray(y, np.float64), -448.0, 448.0).astype(np.float32).astype(ml_dtypes.float8_e4m3fn).view(np.uint8)


def e4m3fn_values(b):
    return E4M3FN[b]


N, D, V = 1024, 1024, 1024


def softmax(v):
    e = np.exp(v - v.max(axis=-1, keepdims=True))
    return e / e.sum(axis=-1, keepdims=True)


def draw0():
    a = mx_kscale(D)
    t = mx_kscale(N)
    c = 0.375 * (V / 384.0) * (32.0 / np.sqrt(N))
    x = bf(np.random.standard_normal((N, D)) * a)
    w_words, w_scales = pack4(np.random.standard_normal((D, V)) / np.sqrt(D) / a[:, None])
    return {
        "x": x,
        "w_words": w_words,
        "w_scales": w_scales,
        "noise": bf(np.random.standard_normal((N, V)) * 1.3),
        "s": bf(c * (1.0 + 0.1 * np.random.standard_normal(N)) * t),
        "xb": bf(np.random.standard_normal((N, D)) / t[:, None]),
        "m": bf(np.random.standard_normal((D, V))),
        "h": bf(np.random.uniform(0.5, 1.5, (D, V))),
    }


def core(x, w_words, w_scales, noise, s, xb, m, h):
    z = mxq(f64(x), 1, "e4m3") @ unpack4(w_words, w_scales)
    p = softmax(z)
    yh = softmax(z + f64(noise))

    r = 384.0 * f64(s)[:, None] * (p - yh)

    gh = (mxq(f64(xb).T, 1, "e4m3") @ mxq(r, 0, "e4m3")) / 32.0

    h1 = 0.6 * f64(h) + 0.4 * gh * gh
    return np.minimum(np.maximum(f64(m) / np.maximum(h1, 0.6), -1.0), 1.0)


def setup_inputs():
    drawn = draw0()
    full = np.asarray(drawn['xb']).astype(np.float64)
    scale = (np.abs(full).reshape(1024, 8, 128).max(axis=(2,)) / 448.0).astype(np.float32)
    given = {}
    for key, value in drawn.items():
        if key == 'xb':
            given['xb_bytes'] = e4m3fn_bytes(full / np.repeat(scale.astype(np.float64), 128, axis=1))
            given['xb_scale'] = scale
        else:
            given[key] = value
    return given


def reference(x, w_words, w_scales, noise, s, xb_bytes, xb_scale, m, h):
    return core(x, w_words, w_scales, noise, s, e4m3fn_values(xb_bytes) * np.repeat(xb_scale.astype(np.float64), 128, axis=1), m, h)

import math
from contextlib import ExitStack

import concourse.mybir as mybir
from concourse.masks import make_identity

F32 = mybir.dt.float32
BF16 = mybir.dt.bfloat16
U32 = mybir.dt.uint32
I32 = mybir.dt.int32
U8 = mybir.dt.uint8
E4X4 = mybir.dt.float8_e4m3fn_x4
E4 = mybir.dt.float8_e4m3fn
FP4X4 = mybir.dt.float4_e2m1fn_x4
ALU = mybir.AluOpType
ACT = mybir.ActivationFunctionType
AX = mybir.AxisListType

N = D = V = 1024
FLOPS = 2 * N * D * V * 2
P = 128


def tile_clippedsquaredcrossproductstep_kernel(tc, x, w_words, w_scales, noise, s, xb_bytes, xb_scale, m, h, out):
    nc = tc.nc
    with ExitStack() as ctx:
        keep = ctx.enter_context(tc.tile_pool(name="keep", bufs=1))
        work = ctx.enter_context(tc.tile_pool(name="work", bufs=2))
        psum = ctx.enter_context(tc.psum_pool(name="psum", bufs=2))

        ws = keep.tile([P, 2, V], U8, name="ws", align_bytes=64)
        wt = keep.tile([P, 2, 2 * V], U8, name="wt", align_bytes=64)
        xr = keep.tile([P, 8, D], BF16, name="xr", align_bytes=64)
        nz = keep.tile([P, 8, V], BF16, name="nz", align_bytes=64)
        xbb = keep.tile([P, 8, D], U8, name="xbb", align_bytes=64)
        xsc = keep.tile([P, 2, 32], F32, name="xsc")
        sb = keep.tile([P, 2, 4], BF16, name="sb")
        mt = keep.tile([P, 8, V], BF16, name="mt", align_bytes=64)
        ht = keep.tile([P, 8, V], BF16, name="ht", align_bytes=64)
        ident = keep.tile([P, P], F32, name="ident")
        s384 = keep.tile([P, 8], F32, name="s384")
        xbc = keep.tile([P, 2, D], U32, name="xbc", align_bytes=64)
        xbs = keep.tile([P, 2, D], U8, name="xbs", align_bytes=64)
        rc = keep.tile([P, 2, V], U32, name="rc", align_bytes=64)
        rs = keep.tile([P, 2, V], U8, name="rs", align_bytes=64)
        e1 = keep.tile([P, 8, V], F32, name="e1", align_bytes=64)
        e2 = keep.tile([P, 8, V], F32, name="e2", align_bytes=64)

        xv = x.rearrange("(g p t) d -> g p t d", p=P, t=4)
        nzv = noise.rearrange("(g p t) v -> g p t v", p=P, t=4)
        xbv = xb_bytes.rearrange("(g p t) d -> g p t d", p=P, t=4)
        hv = h.rearrange("(b p) v -> p b v", p=P)
        mv = m.rearrange("(b p) v -> p b v", p=P)
        dma = nc.sync.dma_start

        ctx.enter_context(tc.manual_schedule())
        make_identity(nc, ident[:])
        nc.vector.memset(ws[:].rearrange("p g n -> p (g n)").bitcast(I32), 0)
        dma(out=xr[:, 0, :], in_=xv[0][:, 0, :])
        dma(out=xsc[:], in_=xb_scale.rearrange("(g p t) j -> p g (t j)", p=P, t=4))
        dma(out=xbb[:, 0:4, :], in_=xbv[0])
        for q in range(4):
            dma(out=ws[32 * q:32 * q + 4, :, :].bitcast(I32), in_=w_scales[:, 4 * q:4 * q + 4, :].rearrange("g r n -> r g n").bitcast(I32))
        for g in range(2):
            dma(out=wt[:, g, :].bitcast(I32), in_=w_words[g].bitcast(I32))
        dma(out=xr[:, 1, :], in_=xv[0][:, 1, :])
        dma(out=nz[:, 0, :], in_=nzv[0][:, 0, :])
        dma(out=xr[:, 2:4, :], in_=xv[0][:, 2:4, :])
        dma(out=nz[:, 1:4, :], in_=nzv[0][:, 1:4, :])
        dma(out=sb[:], in_=s.rearrange("(g p t) -> p g t", p=P, t=4))
        dma(out=xr[:, 4:8, :], in_=xv[1])
        dma(out=nz[:, 4:8, :], in_=nzv[1])
        dma(out=xbb[:, 4:8, :], in_=xbv[1])
        for b in range(0, 8, 4):
            dma(out=ht[:, b:b + 4, :], in_=hv[:, b:b + 4, :])
            dma(out=mt[:, b:b + 4, :], in_=mv[:, b:b + 4, :])

        GZ = (1, 2, 3, 5, 6,)
        xg = {}
        xq = {}
        z = {}
        nm = {}
        st = {}

        def x_turn(i, eng="s"):
            words = xr[:, i, :].bitcast(F32)
            xt = psum.tile([P, 2, 2, P], F32, name="xt", bufs=2)
            for k in range(2):
                for u in range(2):
                    nc.tensor.transpose(xt[:, k, u, :], words[:, 256 * k + u:256 * (k + 1):2], ident[:])
            t_ = work.tile([P, 1024], BF16, name="xg", bufs=3, align_bytes=64)
            o_ = t_[:].bitcast(F32).rearrange("p (k n u) -> p k n u", k=2, u=2)
            if eng == "s":
                nc.scalar.copy(out=o_, in_=xt[:].rearrange("p k u n -> p k n u"))
            else:
                nc.vector.tensor_copy(out=o_, in_=xt[:].rearrange("p k u n -> p k n u"))
            xg[i] = t_

        def x_quant(i):
            xc = work.tile([P, 256], U32, name="xc", bufs=8, align_bytes=64)
            xs = work.tile([P, 256], U8, name="xs", bufs=8, align_bytes=64)
            nc.vector.quantize_mx(out=xc[:].bitcast(E4X4), scales=xs[:], in_=xg[i][:])
            xq[i] = (xc, xs)

        def x_mult(i):
            xc, xs = xq[i]
            for vb in range(2):
                zt = psum.tile([P, 512], F32, name="z", bufs=6)
                for k in range(2):
                    nc.tensor.matmul_mx(
                        out=zt[:],
                        lhsT=xc[:, 128 * k:128 * (k + 1)].bitcast(E4X4),
                        lhsT_scale=xs[:, 128 * k:128 * (k + 1)],
                        rhs=wt[:, k, 1024 * vb:1024 * (vb + 1)].bitcast(FP4X4),
                        rhs_scale=ws[:, k, 512 * vb:512 * (vb + 1)],
                        start=(k == 0), stop=(k == 1))
                z[i, vb] = zt

        def vmax1(i):
            t_ = work.tile([P, 4], F32, name="nm", bufs=8)
            nm[i] = t_
            for vb in range(2):
                vs = slice(512 * vb, 512 * (vb + 1))
                if i in GZ:
                    nc.vector.tensor_scalar(out=e1[:, i, vs], in0=z[i, vb][:], scalar1=-1.0, scalar2=None, op0=ALU.mult, op1=ALU.min, accum_out=t_[:, vb:vb + 1])
                else:
                    nc.vector.tensor_reduce(out=t_[:, vb:vb + 1], in_=z[i, vb][:], axis=AX.X, op=ALU.max, negate=True)

        def zadd(i, vb):
            vs = slice(512 * vb, 512 * (vb + 1))
            if i in GZ:
                if vb == 0:
                    nc.gpsimd.tensor_tensor(out=e2[:, i, :], in0=nz[:, i, :], in1=e1[:, i, :], op=ALU.subtract)
            else:
                nc.vector.tensor_tensor(out=e2[:, i, vs], in0=z[i, vb][:], in1=nz[:, i, vs], op=ALU.add)

        def vnm(i):
            t_ = nm[i]
            nc.vector.tensor_reduce(out=t_[:, 2:3], in_=t_[:, 0:2], axis=AX.X, op=ALU.min)

        def vmax2(i):
            nc.vector.tensor_reduce(out=nm[i][:, 3:4], in_=e2[:, i, :], axis=AX.X, op=ALU.max, negate=True)

        def sexp1(i):
            t_ = work.tile([P, 8], F32, name="st", bufs=8)
            st[i] = t_
            if i in GZ:
                nc.scalar.activation(out=e1[:, i, :], in_=e1[:, i, :], func=ACT.Exp, bias=nm[i][:, 2:3], scale=-1.0, accum_out=t_[:, 2:3])
            else:
                for vb in range(2):
                    vs = slice(512 * vb, 512 * (vb + 1))
                    nc.scalar.activation(out=e1[:, i, vs], in_=z[i, vb][:], func=ACT.Exp, bias=nm[i][:, 2:3], scale=1.0, accum_out=t_[:, vb:vb + 1])

        def sexp2(i):
            nc.scalar.activation(out=e2[:, i, :], in_=e2[:, i, :], func=ACT.Exp, bias=nm[i][:, 3:4], scale=1.0, accum_out=st[i][:, 3:4])

        def vrec_a(i):
            if i not in GZ:
                t_ = st[i]
                nc.vector.tensor_reduce(out=t_[:, 2:3], in_=t_[:, 0:2], axis=AX.X, op=ALU.add)

        def vrec_b(i):
            t_ = st[i]
            nc.vector.reciprocal(out=t_[:, 4:6], in_=t_[:, 2:4])

        def vrec_c(i):
            t_ = st[i]
            nc.vector.tensor_scalar(out=t_[:, 6:8], in0=t_[:, 4:6], scalar1=s384[:, i:i + 1], scalar2=None, op0=ALU.mult)

        def escale(i, col, eng):
            a = e1 if col == 0 else e2
            f = st[i][:, 6 + col:7 + col]
            if eng == "s":
                nc.scalar.activation(out=a[:, i, :], in_=a[:, i, :], func=ACT.Copy, scale=f)
            elif eng == "v":
                nc.vector.tensor_scalar(out=a[:, i, :], in0=a[:, i, :], scalar1=f, scalar2=None, op0=ALU.mult)
            else:
                nc.gpsimd.tensor_scalar(out=a[:, i, :], in0=a[:, i, :], scalar1=f, scalar2=1.0, op0=ALU.mult, op1=ALU.mult)

        rgt = {}

        def vres(g, c):
            rg = work.tile([P, 1024], BF16, name="rg", bufs=3, align_bytes=64)
            vs = slice(256 * c, 256 * (c + 1))
            nc.vector.tensor_tensor(out=rg[:].rearrange("p (v t) -> p v t", t=4),
                                    in0=e1[:, 4 * g:4 * g + 4, vs].rearrange("p t v -> p v t"),
                                    in1=e2[:, 4 * g:4 * g + 4, vs].rearrange("p t v -> p v t"), op=ALU.subtract)
            rgt[g, c] = rg

        def vresq(g, c):
            vs = slice(256 * c, 256 * (c + 1))
            nc.vector.quantize_mx(out=rc[:, g, vs].bitcast(E4X4), scales=rs[:, g, vs], in_=rgt[g, c][:])

        wdt = {}
        xgt = {}

        def xb_wide(q, t, eng):
            g, dh = divmod(q, 2)
            if t == 0:
                wd = work.tile([P, 4, 512], BF16, name="wd", bufs=2)
                wdt[q] = wd
            wd = wdt[q]
            for j in range(4):
                jj = 4 * dh + j
                o_ = wd[:, t, 128 * j:128 * (j + 1)]
                i_ = xbb[:, 4 * g + t, 128 * jj:128 * (jj + 1)].bitcast(E4)
                sc = xsc[:, g, 8 * t + jj:8 * t + jj + 1]
                if eng == "v":
                    nc.vector.tensor_scalar(out=o_, in0=i_, scalar1=sc, scalar2=None, op0=ALU.mult)
                else:
                    nc.scalar.activation(out=o_, in_=i_, func=ACT.Copy, scale=sc)

        def xb_weave(q, eng):
            t_ = work.tile([P, 2048], BF16, name="xbg", bufs=2, align_bytes=64)
            xgt[q] = t_
            o_ = t_[:].rearrange("p (d t) -> p d t", t=4)
            i_ = wdt[q][:].rearrange("p t d -> p d t")
            if eng == "v":
                nc.vector.tensor_copy(out=o_, in_=i_)
            else:
                nc.scalar.copy(out=o_, in_=i_)

        def xb_quant(q):
            g, dh = divmod(q, 2)
            ds_ = slice(512 * dh, 512 * (dh + 1))
            nc.vector.quantize_mx(out=xbc[:, g, ds_].bitcast(E4X4), scales=xbs[:, g, ds_], in_=xgt[q][:])

        U_ENG = "sssssssv"
        W_ENG = "gggggggv"
        for i in range(8):
            x_turn(i)
            if i == 0:
                x_quant(0)
                x_mult(0)
                for t in range(4):
                    xb_wide(0, t, "v")
            elif i == 1:
                x_quant(1)
                x_mult(1)
                xb_weave(0, "v")
                for t in range(4):
                    xb_wide(1, t, "s")
            elif i == 2:
                nc.vector.tensor_scalar(out=s384[:], in0=sb[:].rearrange("p g t -> p (g t)"), scalar1=384.0, scalar2=None, op0=ALU.mult)

        for i in range(11):
            if i < 8:
                vmax1(i)
                zadd(i, 0)
            if i == 0:
                xb_quant(0)
                x_quant(2)
                x_mult(2)
                vnm(0)
                zadd(0, 1)
                x_quant(3)
                x_mult(3)
            if i == 1:
                xb_weave(1, "v")
                vnm(1)
                zadd(1, 1)
                x_quant(4)
                x_mult(4)
                x_quant(5)
                xb_quant(1)
                x_quant(6)
                x_quant(7)
            if i >= 2 and i + 3 < 8:
                x_mult(i + 3)
            if 3 <= i:
                vrec_a(i - 3)
            if 1 <= i < 9:
                sexp1(i - 1)
                vmax2(i - 1)
                sexp2(i - 1)
            if 2 <= i < 8:
                vnm(i)
            if 3 <= i:
                vrec_b(i - 3)
            if 2 <= i < 8:
                zadd(i, 1)
            if 7 <= i < 7 + 4:
                vres(0, i - 7)
            if 3 <= i:
                vrec_c(i - 3)
                escale(i - 3, 0, U_ENG[i - 3])
                escale(i - 3, 1, W_ENG[i - 3])
            if 7 <= i < 7 + 4:
                vresq(0, i - 7)
            if i == 10:
                for t in range(4):
                    xb_wide(2, t, "s")
                xb_weave(2, "s")
        for t in range(4):
            xb_wide(3, t, "s")
        xb_weave(3, "s")
        vres(1, 0)
        vres(1, 1)
        vresq(1, 0)
        xb_quant(2)
        vresq(1, 1)
        vres(1, 2)
        xb_quant(3)

        c_sq = math.sqrt(0.4) / 32.0
        ft = {}

        units = [(0, 512, (0, 1)), (0, 512, (2, 3)), (0, 512, (4, 5)), (0, 512, (6, 7)),
                 (512, 512, (0, 1)), (512, 512, (2, 3)), (512, 512, (4, 5)), (512, 512, (6,)), (512, 512, (7,))]

        def view(t, k):
            v0, w, bs = units[k]
            return t[:, bs[0]:bs[-1] + 1, v0:v0 + w]

        def b_sq(k, j):
            v0, w, bs = units[k]
            if j >= len(bs):
                return
            if j == 0:
                t_ = work.tile([P, len(bs), w], F32, name="f", bufs=6)
                ft[k] = t_
            b = bs[j]
            gt = psum.tile([P, w], F32, name="z", bufs=6)
            for g in range(2):
                nc.tensor.matmul_mx(
                    out=gt[:],
                    lhsT=xbc[:, g, 128 * b:128 * (b + 1)].bitcast(E4X4),
                    lhsT_scale=xbs[:, g, 128 * b:128 * (b + 1)],
                    rhs=rc[:, g, v0:v0 + w].bitcast(E4X4),
                    rhs_scale=rs[:, g, v0:v0 + w],
                    start=(g == 0), stop=(g == 1))
            nc.scalar.activation(out=ft[k][:, j, :], in_=gt[:], func=ACT.Square, scale=c_sq)

        def b_h(k):
            nc.vector.scalar_tensor_tensor(out=ft[k][:], in0=view(ht, k), scalar=0.6, in1=ft[k][:], op0=ALU.mult, op1=ALU.add)

        def b_max(k):
            nc.vector.tensor_scalar(out=ft[k][:], in0=ft[k][:], scalar1=0.6, scalar2=None, op0=ALU.max)

        def b_ars(k):
            nc.scalar.activation(out=ft[k][:], in_=ft[k][:], func=ACT.Abs_reciprocal_sqrt)

        def b_rs(k):
            nc.scalar.activation(out=ft[k][:], in_=ft[k][:], func=ACT.Square)

        def b_mul(k):
            nc.vector.tensor_tensor(out=ft[k][:], in0=ft[k][:], in1=view(mt, k), op=ALU.mult)

        def b_clip(k):
            nc.vector.tensor_scalar(out=ft[k][:], in0=ft[k][:], scalar1=1.0, scalar2=-1.0, op0=ALU.min, op1=ALU.max)
            dma(out=view(out.rearrange("(b p) v -> p b v", p=P), k), in_=ft[k][:])

        n_u = len(units)
        b_sq(0, 0)
        b_sq(0, 1)
        for k in range(n_u + 2):
            b_half = k + 1 < n_u
            if b_half:
                b_sq(k + 1, 0)
            if 1 <= k <= n_u:
                b_ars(k - 1)
            if b_half:
                b_sq(k + 1, 1)
            if 1 <= k <= n_u:
                b_rs(k - 1)
            if k < n_u:
                b_h(k)
            if k == 0:
                vres(1, 3)
                vresq(1, 2)
            if k == 1:
                vresq(1, 3)
            if k >= 2:
                b_mul(k - 2)
            if k < n_u:
                b_max(k)
            if k >= 2:
                b_clip(k - 2)
